import numpy as np
import ml_dtypes


def mxq(x, axis, fmt="e4m3"):
    dtype, down = {"e4m3": (ml_dtypes.float8_e4m3fn, 7), "e5m2": (ml_dtypes.float8_e5m2, 14)}[fmt]
    v = np.moveaxis(np.asarray(x, np.float32).astype(ml_dtypes.bfloat16).astype(np.float64), axis, -1)
    blocks = v.reshape(v.shape[:-1] + (-1, 32))
    amax = np.abs(blocks).max(-1, keepdims=True)
    byte = np.maximum(np.where(amax > 0, np.frexp(amax)[1] - 1 + 127, 0) - down, 1)
    scale = np.exp2(byte - 127.0)
    codes = (blocks / scale).astype(np.float32).astype(dtype).astype(np.float64)
    return np.moveaxis((codes * scale).reshape(v.shape), -1, axis)


WIDE = False


def mx_kscale(k):
    if not WIDE:
        return np.ones(k)
    levels = np.array([10, -10, 5, -5, 0])
    if k % 512:
        return np.exp2(np.random.permutation(np.resize(levels, k // 32))).repeat(32)
    a = np.empty((k // 512, 16))
    for p in range(k // 512):
        a[p, :8] = np.random.permutation(np.resize(levels, 8))
        for g in range(8):
            far = levels[np.abs(levels - a[p, g]) >= 10]
            a[p, g + 8] = far[np.random.randint(len(far))]
    return np.exp2(a.ravel()).repeat(32)


def f64(x):
    return np.asarray(x).astype(np.float64)


def striped(idx):
    return np.tile(idx.reshape(-1, 16).T, (8, 1)).astype(np.uint16)


def unstriped(offs):
    return offs[:16].T.reshape(-1).astype(np.int64)


def pack_weight(w):
    k, n = w.shape
    w = f64(np.asarray(w, np.float32).astype(ml_dtypes.bfloat16)).reshape(k // 32, 32, n)
    amax = np.abs(w).max(1)
    byte = np.clip(np.where(amax > 0, np.frexp(amax)[1] - 1 + 127 - 7, 1), 1, 254)
    scaled = (w * np.exp2(127.0 - byte)[:, None, :]).reshape(k, n).astype(np.float32)
    words = np.ascontiguousarray(scaled.reshape(k // 512, 128, 4, n).transpose(0, 1, 3, 2)).astype(ml_dtypes.float8_e4m3fn).view(np.uint8)
    return words, np.ascontiguousarray(byte.astype(np.uint8).reshape(k // 512, 16, n))


def unpack_weight(words, scales):
    g, p, n, _ = words.shape
    vals = np.ascontiguousarray(words).view(ml_dtypes.float8_e4m3fn).astype(np.float64) * np.repeat(np.exp2(scales.astype(np.float64) - 127.0), 8, axis=1)[..., None]
    return vals.transpose(0, 1, 3, 2).reshape(g * 512, n)


K, T, S, N, H, U = 512, 2048, 512, 256, 512, 1024


def setup_inputs():
    n = np.random.standard_normal
    s = mx_kscale(K)[:, None]
    u = mx_kscale(H)
    packed_xT = pack_weight(n((K, T)) * s)
    return {
        "x_words": packed_xT[0],
        "x_scales": packed_xT[1],
        "w1": (n((K, H)) / np.sqrt(K) / s).astype(np.float32),
        "w2": (n((K, H)) / np.sqrt(K) / s).astype(np.float32),
        "bd": (np.random.uniform(0.2, 1.5, (H, U))).astype(np.float32),
        "unit": (np.random.uniform(0.6, 1.4, (H, 1)) * u[:, None]).astype(np.float32),
        "w3": (n((H, N)) / np.sqrt(H) / u[:, None]).astype(np.float32),
        "offs": striped(np.random.permutation(T)[:S]),
        "l1": striped(np.random.permutation(np.concatenate([np.arange(S), np.random.randint(0, S, U - S)]))),
        "r1": striped(np.random.permutation(np.concatenate([np.arange(S), np.random.randint(0, S, U - S)]))),
    }


def reference(x_words, x_scales, w1, w2, bd, unit, w3, offs, l1, r1):
    xq = unpack_weight(x_words, x_scales)[:, unstriped(offs)]
    y = mxq(f64(w1), 0, "e4m3").T @ xq
    yl = y[:, unstriped(l1)]
    yr = y[:, unstriped(r1)]
    dif = np.abs(yl - yr)
    z1 = mxq(f64(w2), 0, "e4m3").T @ xq
    zl = z1[:, unstriped(l1)]
    zr = z1[:, unstriped(r1)]
    hid = f64(unit) * (dif * f64(bd) + np.minimum(zl, zr))
    return mxq(f64(w3), 0, "e4m3").T @ mxq(hid, 0, "e4m3")

@@ -1,0 +1,212 @@
+from contextlib import ExitStack
+
+import concourse.mybir as mybir
+
+K, T, S, N, H, U = 512, 2048, 512, 256, 512, 1024
+FLOPS = 2 * K * H * S * 2 + 2 * H * N * U
+
+F32 = mybir.dt.float32
+BF16 = mybir.dt.bfloat16
+I32 = mybir.dt.int32
+U32 = mybir.dt.uint32
+U16 = mybir.dt.uint16
+U8 = mybir.dt.uint8
+FP8X4 = mybir.dt.float8_e4m3fn_x4
+ALU = mybir.AluOpType
+ACT = mybir.ActivationFunctionType
+
+P = 128
+PACK = 4
+LIST = 16
+GROUPS = ((0, 512), (512, 512))
+CHUNKS = ((0, 256, True), (256, 256, False), (512, 256, False), (768, 128, False), (896, 128, False))
+T_STEP = 4
+Y_WINDOW = 1024
+Z_WINDOW = 512
+Y_ON_VECTOR = (1, 2, 3)
+Z_ON_VECTOR = (1, 3)
+
+
+def tile_picked_ysegmrg_len_p_kernel(
+    tc, x_words, x_scales, w1, w2, bd, unit, w3, offs, l1, r1, out
+):
+    nc = tc.nc
+    W2B = nc.scalar.copy
+    with ExitStack() as ctx:
+        lists = ctx.enter_context(tc.tile_pool(name="lists", bufs=1))
+        keep = ctx.enter_context(tc.tile_pool(name="keep", bufs=1))
+        proj_psum = ctx.enter_context(tc.psum_pool(name="proj_psum", bufs=5))
+        out_psum = ctx.enter_context(tc.psum_pool(name="out_psum", bufs=3))
+
+        offs_sb = lists.tile([P, S // LIST], U16, name="offs_sb")
+        l_sb = lists.tile([P, U // LIST], U16, name="l_sb")
+        r_sb = lists.tile([P, U // LIST], U16, name="r_sb")
+
+        xw = keep.tile([P, T], I32, name="xw", align_bytes=64)
+        xs = keep.tile([P, T], U8, name="xs", align_bytes=64)
+        w1_raw = keep.tile([P, PACK, H], F32, name="w1_raw", align_bytes=64)
+        w2_raw = keep.tile([P, PACK, H], F32, name="w2_raw", align_bytes=64)
+        w3_raw = keep.tile([P, PACK, N], F32, name="w3_raw", align_bytes=64)
+        unit_sb = keep.tile([P, PACK], F32, name="unit_sb")
+        bd_sb = [keep.tile([P, PACK, w], F32, name="bd%d" % c, align_bytes=64) for c, (c0, w) in enumerate(GROUPS)]
+        bd_rows = bd.rearrange("(p t) r -> p t r", t=PACK)
+
+        xs_in = keep.tile([P, T // 4], I32, name="xs_in", align_bytes=64)
+        nc.vector.memset(xs[:].bitcast(I32), 0)
+        for q in range(4):
+            nc.sync.dma_start(out=xs_in[32 * q : 32 * q + 4, :], in_=x_scales[0, 4 * q : 4 * q + 4, :].bitcast(I32))
+        nc.sync.dma_start(offs_sb[:], offs)
+        nc.sync.dma_start(out=w1_raw[:], in_=w1.rearrange("(p j) c -> p j c", j=PACK))
+        nc.sync.dma_start(out=xw[:], in_=x_words[0].rearrange("p n t -> p (n t)").bitcast(I32))
+        nc.scalar.dma_start(out=unit_sb[:], in_=unit.rearrange("(p t) o -> p (t o)", t=PACK))
+        nc.sync.dma_start(l_sb[:], l1)
+        nc.sync.dma_start(r_sb[:], r1)
+        for q in range(4):
+            nc.vector.tensor_copy(xs[32 * q : 32 * q + 4, :].bitcast(I32), xs_in[32 * q : 32 * q + 4, :])
+        nc.sync.dma_start(out=w2_raw[:], in_=w2.rearrange("(p j) c -> p j c", j=PACK))
+        for c, (c0, w) in enumerate(GROUPS):
+            nc.sync.dma_start(out=bd_sb[c][:], in_=bd_rows[:, :, c0 : c0 + w])
+            if c == 0:
+                nc.sync.dma_start(out=w3_raw[:], in_=w3.rearrange("(p j) c -> p j c", j=PACK))
+
+        mag = keep.tile([P, PACK], F32, name="mag")
+        neg = keep.tile([P, PACK], F32, name="neg")
+        sign = keep.tile([P, PACK], F32, name="sign")
+        nc.scalar.activation(mag[:], unit_sb[:], ACT.Abs)
+        nc.vector.tensor_scalar(neg[:], unit_sb[:], 0.0, -2.0, ALU.is_lt, ALU.mult)
+        nc.vector.tensor_scalar(sign[:], neg[:], 1.0, None, ALU.add)
+
+        def cast_pair(raw, name, half, copy):
+            g = keep.tile([P, 2, P, PACK], BF16, name="%s_bf%d" % (name, half), align_bytes=64)
+            copy(
+                g[:].rearrange("p t m j -> p m j t"),
+                raw[:].rearrange("p j (m h t) -> p h m j t", h=2, t=2)[:, half],
+            )
+            return g
+
+        def quantize(g_flat, width, name):
+            codes = keep.tile([P, width], U32, name=name + "_codes", align_bytes=64)
+            scales = keep.tile([P, width], U8, name=name + "_scales", align_bytes=64)
+            nc.vector.quantize_mx(out=codes[:].bitcast(FP8X4), scales=scales[:], in_=g_flat)
+            return codes, scales
+
+        gs = keep.tile([P, S], U8, name="gs", align_bytes=64)
+        gw = keep.tile([P, S], U32, name="gw", align_bytes=64)
+        nc.vector.tensor_copy(gs[:], xs[:].indirect(offs_sb[:]))
+        g1 = [cast_pair(w1_raw, "w1", 0, nc.vector.tensor_copy), cast_pair(w1_raw, "w1", 1, nc.scalar.copy)]
+        q1 = [quantize(g[:].rearrange("p t m j -> p (t m j)"), 2 * P, "w1q%d" % h) for h, g in enumerate(g1)]
+        nc.vector.tensor_copy(gw[:], xw[:].bitcast(U32).indirect(offs_sb[:]))
+
+        y = [keep.tile([P, Y_WINDOW], F32, name="y%d" % t, align_bytes=64) for t in range(PACK)]
+        z = [keep.tile([P, Z_WINDOW], F32, name="z%d" % t, align_bytes=64) for t in range(PACK)]
+        for win in y + z:
+            if win.shape[1] > S:
+                nc.vector.memset(win[:, S:], 0.0)
+
+        def project(q, t, win, on_vector):
+            codes, scales = q[t // 2]
+            cols = slice((t % 2) * P, (t % 2 + 1) * P)
+            acc = proj_psum.tile([P, S], F32, name="acc")
+            nc.tensor.matmul_mx(
+                out=acc[:], lhsT=codes[:, cols].bitcast(FP8X4), lhsT_scale=scales[:, cols],
+                rhs=gw[:].bitcast(FP8X4), rhs_scale=gs[:], start=True, stop=True,
+            )
+            if on_vector:
+                nc.vector.tensor_scalar(win[:, :S], acc[:], mag[:, t : t + 1], None, ALU.mult)
+            else:
+                nc.scalar.activation(win[:, :S], acc[:], ACT.Copy, scale=mag[:, t : t + 1])
+
+        def work(name, c, w):
+            return keep.tile([P, PACK, w], F32, name="%s%d" % (name, c), align_bytes=64)
+
+        def entries(lst, c0, w):
+            return lst[:, c0 // LIST : (c0 + w) // LIST]
+
+        n_ch = len(CHUNKS)
+        yl = [work("yl", g, w) for g, (c0, w) in enumerate(GROUPS)]
+        dif = [work("dif", g, w) for g, (c0, w) in enumerate(GROUPS)]
+        zl = [work("zl", c, w) for c, (c0, w, f) in enumerate(CHUNKS)]
+        zr = [work("zr", c, w) for c, (c0, w, f) in enumerate(CHUNKS)]
+
+        def y_pairs(g):
+            c0, w = GROUPS[g]
+            for t in range(PACK):
+                nc.scalar.activation(yl[g][:, t, :], y[t][:].indirect(entries(l_sb, c0, w)), ACT.Copy)
+                nc.vector.tensor_tensor(dif[g][:, t, :], y[t][:].indirect(entries(r_sb, c0, w)), yl[g][:, t, :], ALU.subtract)
+
+        def length_term(g):
+            for t in range(0, PACK, T_STEP):
+                part = dif[g][:, t : t + T_STEP, :]
+                nc.scalar.activation(part, part, ACT.Abs)
+                nc.vector.tensor_tensor(part, part, bd_sb[g][:, t : t + T_STEP, :], ALU.mult)
+
+        def term(c):
+            c0, w, f = CHUNKS[c]
+            g = [k for k, (g0, gw_) in enumerate(GROUPS) if g0 <= c0 < g0 + gw_][0]
+            return dif[g][:, :, c0 - GROUPS[g][0] : c0 - GROUPS[g][0] + w]
+
+        def z_sides(c):
+            c0, w, f = CHUNKS[c]
+            for t in range(PACK):
+                for dst, lst in ((zl, l_sb), (zr, r_sb)):
+                    win = z[t][:].indirect(entries(lst, c0, w))
+                    if f:
+                        nc.vector.tensor_tensor(dst[c][:, t, :], win, term(c)[:, t, :], ALU.add)
+                    else:
+                        nc.scalar.activation(dst[c][:, t, :], win, ACT.Copy)
+
+        hid = [keep.tile([P, w, PACK], BF16, name="hid%d" % c, align_bytes=64) for c, (c0, w, f) in enumerate(CHUNKS)]
+
+        def combine(c):
+            walk = "p t (c i) -> p c t i"
+            dst = hid[c][:].rearrange("p (c i) t -> p c t i", i=2)
+            if CHUNKS[c][2]:
+                nc.vector.tensor_tensor(dst, zl[c][:].rearrange(walk, i=2), zr[c][:].rearrange(walk, i=2), ALU.min)
+            else:
+                nc.vector.tensor_tensor(zl[c][:], zl[c][:], zr[c][:], ALU.min)
+                nc.vector.tensor_tensor(dst, zl[c][:].rearrange(walk, i=2), term(c).rearrange(walk, i=2), ALU.add)
+
+        out_rows = out.rearrange("(h p) r -> p h r", p=P)
+
+        def finish(c):
+            c0, w, f = CHUNKS[c]
+            codes, scales = quantize(hid[c][:].rearrange("p r t -> p (r t)"), w, "hq%d" % c)
+            acc = out_psum.tile([P, 2, w], F32, name="oacc")
+            for h in range(2):
+                cols = slice(h * P, (h + 1) * P)
+                nc.tensor.matmul_mx(
+                    out=acc[:, h, :], lhsT=q3[0][:, cols].bitcast(FP8X4), lhsT_scale=q3[1][:, cols],
+                    rhs=codes[:].bitcast(FP8X4), rhs_scale=scales[:], start=True, stop=True,
+                )
+            res = keep.tile([P, 2, w], F32, name="res%d" % c, align_bytes=64)
+            nc.scalar.copy(res[:], acc[:])
+            nc.sync.dma_start(out=out_rows[:, :, c0 : c0 + w], in_=res[:])
+
+        for t in range(PACK):
+            project(q1, t, y[t], t in Y_ON_VECTOR)
+        y_pairs(0)
+        g2 = [cast_pair(w2_raw, "w2", 0, nc.vector.tensor_copy), cast_pair(w2_raw, "w2", 1, W2B)]
+        q2 = [quantize(g[:].rearrange("p t m j -> p (t m j)"), 2 * P, "w2q%d" % h) for h, g in enumerate(g2)]
+        for t in range(PACK):
+            project(q2, t, z[t], t in Z_ON_VECTOR)
+        g3 = keep.tile([P, N, PACK], BF16, name="w3_bf", align_bytes=64)
+        c = 0
+        for g, (g0, gwidth) in enumerate(GROUPS):
+            length_term(g)
+            if g + 1 < len(GROUPS):
+                y_pairs(g + 1)
+            if g == 0:
+                nc.vector.tensor_tensor(
+                    g3[:].rearrange("p (c i) j -> p c j i", i=2),
+                    w3_raw[:].rearrange("p j (c i) -> p c j i", i=2),
+                    sign[:].unsqueeze(1).unsqueeze(3).broadcast_to([P, N // 2, PACK, 2]),
+                    ALU.mult,
+                )
+                q3 = quantize(g3[:].rearrange("p n j -> p (n j)"), N, "w3q")
+            while c < n_ch and CHUNKS[c][0] < g0 + gwidth:
+                z_sides(c)
+                if c > 0:
+                    finish(c - 1)
+                combine(c)
+                c += 1
+        finish(n_ch - 1)

@@ -19,19 +19,29 @@ P = 128
 PACK = 4
 LIST = 16
 GROUPS = ((0, 512), (512, 512))
-CHUNKS = ((0, 256, True), (256, 256, False), (512, 256, False), (768, 128, False), (896, 128, False))
+UNITS = ((0, 256, True), (256, 256, False), (512, 256, False), (768, 192, False), (960, 64, False))
+CHUNKS = ((0, 256), (256, 256), (512, 256), (768, 128), (896, 64), (960, 64))
+AHEAD = 512
+FUSED = 256
+TERM_AT = 0
+PIN = "zp"
+W1B = 1
+W3_FIRST = False
+X_PARTS = 2
+RUN = 4
+OUT_ON_VECTOR = ()
 T_STEP = 4
 Y_WINDOW = 1024
 Z_WINDOW = 512
-Y_ON_VECTOR = (1, 2, 3)
-Z_ON_VECTOR = (1, 3)
+Y_ON_VECTOR = (1, 3)
+Z_ON_VECTOR = (3,)
 
 
 def tile_picked_ysegmrg_len_p_kernel(
     tc, x_words, x_scales, w1, w2, bd, unit, w3, offs, l1, r1, out
 ):
     nc = tc.nc
-    W2B = nc.scalar.copy
+    W2B = nc.vector.tensor_copy
     with ExitStack() as ctx:
         lists = ctx.enter_context(tc.tile_pool(name="lists", bufs=1))
         keep = ctx.enter_context(tc.tile_pool(name="keep", bufs=1))
@@ -63,10 +73,12 @@ def tile_picked_ysegmrg_len_p_kernel(
         nc.sync.dma_start(r_sb[:], r1)
         for q in range(4):
             nc.vector.tensor_copy(xs[32 * q : 32 * q + 4, :].bitcast(I32), xs_in[32 * q : 32 * q + 4, :])
+        if W3_FIRST:
+            nc.sync.dma_start(out=w3_raw[:], in_=w3.rearrange("(p j) c -> p j c", j=PACK))
         nc.sync.dma_start(out=w2_raw[:], in_=w2.rearrange("(p j) c -> p j c", j=PACK))
         for c, (c0, w) in enumerate(GROUPS):
             nc.sync.dma_start(out=bd_sb[c][:], in_=bd_rows[:, :, c0 : c0 + w])
-            if c == 0:
+            if c == 0 and not W3_FIRST:
                 nc.sync.dma_start(out=w3_raw[:], in_=w3.rearrange("(p j) c -> p j c", j=PACK))
 
         mag = keep.tile([P, PACK], F32, name="mag")
@@ -95,22 +107,25 @@ def tile_picked_ysegmrg_len_p_kernel(
         nc.vector.tensor_copy(gs[:], xs[:].indirect(offs_sb[:]))
         g1 = [cast_pair(w1_raw, "w1", 0, nc.vector.tensor_copy), cast_pair(w1_raw, "w1", 1, nc.scalar.copy)]
         q1 = [quantize(g[:].rearrange("p t m j -> p (t m j)"), 2 * P, "w1q%d" % h) for h, g in enumerate(g1)]
-        nc.vector.tensor_copy(gw[:], xw[:].bitcast(U32).indirect(offs_sb[:]))
+        halves = [slice(h * S // X_PARTS, (h + 1) * S // X_PARTS) for h in range(X_PARTS)]
+        for cols in halves:
+            nc.vector.tensor_copy(gw[:, cols], xw[:].bitcast(U32).indirect(offs_sb[:, cols.start // LIST : cols.stop // LIST]))
 
         y = [keep.tile([P, Y_WINDOW], F32, name="y%d" % t, align_bytes=64) for t in range(PACK)]
         z = [keep.tile([P, Z_WINDOW], F32, name="z%d" % t, align_bytes=64) for t in range(PACK)]
         for win in y + z:
             if win.shape[1] > S:
-                nc.vector.memset(win[:, S:], 0.0)
+                nc.gpsimd.memset(win[:, S:], 0.0)
 
-        def project(q, t, win, on_vector):
+        def multiply(q, t, acc, part):
             codes, scales = q[t // 2]
             cols = slice((t % 2) * P, (t % 2 + 1) * P)
-            acc = proj_psum.tile([P, S], F32, name="acc")
             nc.tensor.matmul_mx(
-                out=acc[:], lhsT=codes[:, cols].bitcast(FP8X4), lhsT_scale=scales[:, cols],
-                rhs=gw[:].bitcast(FP8X4), rhs_scale=gs[:], start=True, stop=True,
+                out=acc[:, part], lhsT=codes[:, cols].bitcast(FP8X4), lhsT_scale=scales[:, cols],
+                rhs=gw[:, part].bitcast(FP8X4), rhs_scale=gs[:, part], start=True, stop=True,
             )
+
+        def leave(acc, t, win, on_vector):
             if on_vector:
                 nc.vector.tensor_scalar(win[:, :S], acc[:], mag[:, t : t + 1], None, ALU.mult)
             else:
@@ -124,9 +139,9 @@ def tile_picked_ysegmrg_len_p_kernel(
 
         n_ch = len(CHUNKS)
         yl = [work("yl", g, w) for g, (c0, w) in enumerate(GROUPS)]
-        dif = [work("dif", g, w) for g, (c0, w) in enumerate(GROUPS)]
-        zl = [work("zl", c, w) for c, (c0, w, f) in enumerate(CHUNKS)]
-        zr = [work("zr", c, w) for c, (c0, w, f) in enumerate(CHUNKS)]
+        dif = [keep.tile([P, PACK, w], F32, name="dif%d" % g, tag="dif%d" % g, align_bytes=64) for g, (c0, w) in enumerate(GROUPS)]
+        term = [work("term", g, w) for g, (c0, w) in enumerate(GROUPS)]
+        zl, zr = [], []
 
         def y_pairs(g):
             c0, w = GROUPS[g]
@@ -134,42 +149,43 @@ def tile_picked_ysegmrg_len_p_kernel(
                 nc.scalar.activation(yl[g][:, t, :], y[t][:].indirect(entries(l_sb, c0, w)), ACT.Copy)
                 nc.vector.tensor_tensor(dif[g][:, t, :], y[t][:].indirect(entries(r_sb, c0, w)), yl[g][:, t, :], ALU.subtract)
 
-        def length_term(g):
-            for t in range(0, PACK, T_STEP):
-                part = dif[g][:, t : t + T_STEP, :]
-                nc.scalar.activation(part, part, ACT.Abs)
-                nc.vector.tensor_tensor(part, part, bd_sb[g][:, t : t + T_STEP, :], ALU.mult)
+        def magnitude(g):
+            nc.scalar.activation(term[g][:], dif[g][:], ACT.Abs)
 
-        def term(c):
-            c0, w, f = CHUNKS[c]
-            g = [k for k, (g0, gw_) in enumerate(GROUPS) if g0 <= c0 < g0 + gw_][0]
-            return dif[g][:, :, c0 - GROUPS[g][0] : c0 - GROUPS[g][0] + w]
+        def times_length(g):
+            nc.vector.tensor_tensor(term[g][:], term[g][:], bd_sb[g][:], ALU.mult)
 
-        def z_sides(c):
-            c0, w, f = CHUNKS[c]
+        def columns(tiles, ranges, c0, w):
+            k = [k for k, r in enumerate(ranges) if r[0] <= c0 < r[0] + r[1]][0]
+            return tiles[k][:, :, c0 - ranges[k][0] : c0 - ranges[k][0] + w]
+
+        def z_sides(u):
+            c0, w, f = UNITS[u]
             for t in range(PACK):
                 for dst, lst in ((zl, l_sb), (zr, r_sb)):
                     win = z[t][:].indirect(entries(lst, c0, w))
                     if f:
-                        nc.vector.tensor_tensor(dst[c][:, t, :], win, term(c)[:, t, :], ALU.add)
+                        nc.vector.tensor_tensor(dst[u][:, t, :], win, columns(term, GROUPS, c0, w)[:, t, :], ALU.add)
                     else:
-                        nc.scalar.activation(dst[c][:, t, :], win, ACT.Copy)
+                        nc.scalar.activation(dst[u][:, t, :], win, ACT.Copy)
 
-        hid = [keep.tile([P, w, PACK], BF16, name="hid%d" % c, align_bytes=64) for c, (c0, w, f) in enumerate(CHUNKS)]
+        hid = [keep.tile([P, w, PACK], BF16, name="hid%d" % c, align_bytes=64) for c, (c0, w) in enumerate(CHUNKS)]
 
-        def combine(c):
+        def combine(c, f):
+            c0, w = CHUNKS[c]
             walk = "p t (c i) -> p c t i"
-            dst = hid[c][:].rearrange("p (c i) t -> p c t i", i=2)
-            if CHUNKS[c][2]:
-                nc.vector.tensor_tensor(dst, zl[c][:].rearrange(walk, i=2), zr[c][:].rearrange(walk, i=2), ALU.min)
+            dst = hid[c][:].rearrange("p (c i) t -> p c t i", i=RUN)
+            left = columns(zl, UNITS, c0, w)
+            if f:
+                nc.vector.tensor_tensor(dst, left.rearrange(walk, i=RUN), columns(zr, UNITS, c0, w).rearrange(walk, i=RUN), ALU.min)
             else:
-                nc.vector.tensor_tensor(zl[c][:], zl[c][:], zr[c][:], ALU.min)
-                nc.vector.tensor_tensor(dst, zl[c][:].rearrange(walk, i=2), term(c).rearrange(walk, i=2), ALU.add)
+                nc.vector.tensor_tensor(left, left, columns(zr, UNITS, c0, w), ALU.min)
+                nc.vector.tensor_tensor(dst, left.rearrange(walk, i=RUN), columns(term, GROUPS, c0, w).rearrange(walk, i=RUN), ALU.add)
 
         out_rows = out.rearrange("(h p) r -> p h r", p=P)
 
         def finish(c):
-            c0, w, f = CHUNKS[c]
+            c0, w = CHUNKS[c]
             codes, scales = quantize(hid[c][:].rearrange("p r t -> p (r t)"), w, "hq%d" % c)
             acc = out_psum.tile([P, 2, w], F32, name="oacc")
             for h in range(2):
@@ -179,34 +195,58 @@ def tile_picked_ysegmrg_len_p_kernel(
                     rhs=codes[:].bitcast(FP8X4), rhs_scale=scales[:], start=True, stop=True,
                 )
             res = keep.tile([P, 2, w], F32, name="res%d" % c, align_bytes=64)
-            nc.scalar.copy(res[:], acc[:])
+            if c in OUT_ON_VECTOR:
+                nc.vector.tensor_copy(res[:], acc[:])
+            else:
+                nc.scalar.copy(res[:], acc[:])
             nc.sync.dma_start(out=out_rows[:, :, c0 : c0 + w], in_=res[:])
 
+        accs = [proj_psum.tile([P, S], F32, name="acc") for t in range(PACK)]
         for t in range(PACK):
-            project(q1, t, y[t], t in Y_ON_VECTOR)
+            for part in halves:
+                multiply(q1, t, accs[t], part)
+        g3 = keep.tile([P, N, PACK], BF16, name="w3_bf", align_bytes=64)
+        for t in range(PACK):
+            leave(accs[t], t, y[t], t in Y_ON_VECTOR)
         y_pairs(0)
+        def prep3():
+            nc.vector.tensor_tensor(
+                g3[:].rearrange("p (c i) j -> p c j i", i=2),
+                w3_raw[:].rearrange("p j (c i) -> p c j i", i=2),
+                sign[:].unsqueeze(1).unsqueeze(3).broadcast_to([P, N // 2, PACK, 2]),
+                ALU.mult,
+            )
+            return quantize(g3[:].rearrange("p n j -> p (n j)"), N, "w3q")
+
+        if W3_FIRST:
+            q3 = prep3()
         g2 = [cast_pair(w2_raw, "w2", 0, nc.vector.tensor_copy), cast_pair(w2_raw, "w2", 1, W2B)]
         q2 = [quantize(g[:].rearrange("p t m j -> p (t m j)"), 2 * P, "w2q%d" % h) for h, g in enumerate(g2)]
         for t in range(PACK):
-            project(q2, t, z[t], t in Z_ON_VECTOR)
-        g3 = keep.tile([P, N, PACK], BF16, name="w3_bf", align_bytes=64)
+            acc = proj_psum.tile([P, S], F32, name="acc")
+            multiply(q2, t, acc, slice(0, S))
+            leave(acc, t, z[t], t in Z_ON_VECTOR)
+        magnitude(0)
+        y_pairs(1)
+        times_length(0)
+        if not W3_FIRST:
+            q3 = prep3()
+        magnitude(1)
+        fused = keep.tile([P, 2 * PACK * FUSED], F32, name="zf", align_bytes=64)
+        plain = keep.tile([P, 2 * PACK * (U - FUSED)], F32, name="zp", tag=PIN, align_bytes=64)
+        for u0, uw, f in UNITS:
+            base, at = (fused, u0) if f else (plain, u0 - FUSED)
+            at = 2 * PACK * at
+            zl.append(base[:, at : at + PACK * uw].rearrange("p (t r) -> p t r", t=PACK))
+            zr.append(base[:, at + PACK * uw : at + 2 * PACK * uw].rearrange("p (t r) -> p t r", t=PACK))
         c = 0
-        for g, (g0, gwidth) in enumerate(GROUPS):
-            length_term(g)
-            if g + 1 < len(GROUPS):
-                y_pairs(g + 1)
-            if g == 0:
-                nc.vector.tensor_tensor(
-                    g3[:].rearrange("p (c i) j -> p c j i", i=2),
-                    w3_raw[:].rearrange("p j (c i) -> p c j i", i=2),
-                    sign[:].unsqueeze(1).unsqueeze(3).broadcast_to([P, N // 2, PACK, 2]),
-                    ALU.mult,
-                )
-                q3 = quantize(g3[:].rearrange("p n j -> p (n j)"), N, "w3q")
-            while c < n_ch and CHUNKS[c][0] < g0 + gwidth:
-                z_sides(c)
+        for u, (u0, uw, f) in enumerate(UNITS):
+            z_sides(u)
+            if u == TERM_AT:
+                times_length(1)
+            while c < n_ch and CHUNKS[c][0] < u0 + uw:
+                combine(c, f)
                 if c > 0:
                     finish(c - 1)
-                combine(c)
                 c += 1
         finish(n_ch - 1)

@@ -3,7 +3,7 @@ from contextlib import ExitStack
 import concourse.mybir as mybir
 
 K, T, S, N, H, U = 512, 2048, 512, 256, 512, 1024
-FLOPS = 2 * K * H * S * 2 + 2 * H * N * U
+FLOPS = 2 * (2 * K * H * S) + 2 * H * N * U
 
 F32 = mybir.dt.float32
 BF16 = mybir.dt.bfloat16
@@ -17,236 +17,245 @@ ACT = mybir.ActivationFunctionType
 
 P = 128
 PACK = 4
+QUADRANT = 32
 LIST = 16
-GROUPS = ((0, 512), (512, 512))
-UNITS = ((0, 256, True), (256, 256, False), (512, 256, False), (768, 192, False), (960, 64, False))
-CHUNKS = ((0, 256), (256, 256), (512, 256), (768, 128), (896, 64), (960, 64))
-AHEAD = 512
-FUSED = 256
-TERM_AT = 0
-PIN = "zp"
-W1B = 1
-W3_FIRST = False
-X_PARTS = 2
 RUN = 4
-OUT_ON_VECTOR = ()
-T_STEP = 4
-Y_WINDOW = 1024
-Z_WINDOW = 512
-Y_ON_VECTOR = (1, 3)
-Z_ON_VECTOR = (3,)
+
+GROUP = 512
+STEP = 256
+LAST = 64
+FUSED = 256
+Z_ON_SCALAR = 3
+
+Y_RANGES = [(first, GROUP) for first in range(0, U, GROUP)]
+Z_RANGES = [(first, STEP) for first in range(0, U - STEP, STEP)] + [(U - STEP, STEP - LAST), (U - LAST, LAST)]
+OUT_RANGES = Z_RANGES[:-2] + [(U - STEP, STEP - 2 * LAST), (U - 2 * LAST, LAST), (U - LAST, LAST)]
 
 
 def tile_picked_ysegmrg_len_p_kernel(
     tc, x_words, x_scales, w1, w2, bd, unit, w3, offs, l1, r1, out
 ):
     nc = tc.nc
-    W2B = nc.vector.tensor_copy
     with ExitStack() as ctx:
         lists = ctx.enter_context(tc.tile_pool(name="lists", bufs=1))
         keep = ctx.enter_context(tc.tile_pool(name="keep", bufs=1))
-        proj_psum = ctx.enter_context(tc.psum_pool(name="proj_psum", bufs=5))
+        proj_psum = ctx.enter_context(tc.psum_pool(name="proj_psum", bufs=PACK + 1))
         out_psum = ctx.enter_context(tc.psum_pool(name="out_psum", bufs=3))
 
+        def sbuf(name, shape, dtype):
+            return keep.tile([P] + shape, dtype, name=name, align_bytes=64)
+
         offs_sb = lists.tile([P, S // LIST], U16, name="offs_sb")
-        l_sb = lists.tile([P, U // LIST], U16, name="l_sb")
-        r_sb = lists.tile([P, U // LIST], U16, name="r_sb")
-
-        xw = keep.tile([P, T], I32, name="xw", align_bytes=64)
-        xs = keep.tile([P, T], U8, name="xs", align_bytes=64)
-        w1_raw = keep.tile([P, PACK, H], F32, name="w1_raw", align_bytes=64)
-        w2_raw = keep.tile([P, PACK, H], F32, name="w2_raw", align_bytes=64)
-        w3_raw = keep.tile([P, PACK, N], F32, name="w3_raw", align_bytes=64)
+        left_sb = lists.tile([P, U // LIST], U16, name="left_sb")
+        right_sb = lists.tile([P, U // LIST], U16, name="right_sb")
+        x_table = sbuf("x_table", [T], I32)
+        scale_table = sbuf("scale_table", [T], U8)
+        w1_raw = sbuf("w1_raw", [PACK, H], F32)
+        w2_raw = sbuf("w2_raw", [PACK, H], F32)
+        w3_raw = sbuf("w3_raw", [PACK, N], F32)
         unit_sb = keep.tile([P, PACK], F32, name="unit_sb")
-        bd_sb = [keep.tile([P, PACK, w], F32, name="bd%d" % c, align_bytes=64) for c, (c0, w) in enumerate(GROUPS)]
-        bd_rows = bd.rearrange("(p t) r -> p t r", t=PACK)
+        bd_sb = [sbuf("bd%d" % g, [PACK, GROUP], F32) for g in range(len(Y_RANGES))]
+        scale_rows = sbuf("scale_rows", [T // 4], I32)
 
-        xs_in = keep.tile([P, T // 4], I32, name="xs_in", align_bytes=64)
-        nc.vector.memset(xs[:].bitcast(I32), 0)
-        for q in range(4):
-            nc.sync.dma_start(out=xs_in[32 * q : 32 * q + 4, :], in_=x_scales[0, 4 * q : 4 * q + 4, :].bitcast(I32))
+        nc.vector.memset(scale_table[:].bitcast(I32), 0)
+        live_rows = [slice(QUADRANT * q, QUADRANT * q + 4) for q in range(P // QUADRANT)]
+        for q, rows in enumerate(live_rows):
+            nc.sync.dma_start(out=scale_rows[rows, :], in_=x_scales[0, 4 * q : 4 * q + 4, :].bitcast(I32))
         nc.sync.dma_start(offs_sb[:], offs)
         nc.sync.dma_start(out=w1_raw[:], in_=w1.rearrange("(p j) c -> p j c", j=PACK))
-        nc.sync.dma_start(out=xw[:], in_=x_words[0].rearrange("p n t -> p (n t)").bitcast(I32))
+        nc.sync.dma_start(out=x_table[:], in_=x_words[0].rearrange("p n j -> p (n j)").bitcast(I32))
         nc.scalar.dma_start(out=unit_sb[:], in_=unit.rearrange("(p t) o -> p (t o)", t=PACK))
-        nc.sync.dma_start(l_sb[:], l1)
-        nc.sync.dma_start(r_sb[:], r1)
-        for q in range(4):
-            nc.vector.tensor_copy(xs[32 * q : 32 * q + 4, :].bitcast(I32), xs_in[32 * q : 32 * q + 4, :])
-        if W3_FIRST:
-            nc.sync.dma_start(out=w3_raw[:], in_=w3.rearrange("(p j) c -> p j c", j=PACK))
+        nc.sync.dma_start(left_sb[:], l1)
+        nc.sync.dma_start(right_sb[:], r1)
+        for rows in live_rows:
+            nc.vector.tensor_copy(scale_table[rows, :].bitcast(I32), scale_rows[rows, :])
         nc.sync.dma_start(out=w2_raw[:], in_=w2.rearrange("(p j) c -> p j c", j=PACK))
-        for c, (c0, w) in enumerate(GROUPS):
-            nc.sync.dma_start(out=bd_sb[c][:], in_=bd_rows[:, :, c0 : c0 + w])
-            if c == 0 and not W3_FIRST:
-                nc.sync.dma_start(out=w3_raw[:], in_=w3.rearrange("(p j) c -> p j c", j=PACK))
+        bd_planes = bd.rearrange("(p t) r -> p t r", t=PACK)
+        nc.sync.dma_start(out=bd_sb[0][:], in_=bd_planes[:, :, :GROUP])
+        nc.sync.dma_start(out=w3_raw[:], in_=w3.rearrange("(p j) c -> p j c", j=PACK))
+        nc.sync.dma_start(out=bd_sb[1][:], in_=bd_planes[:, :, GROUP:])
 
-        mag = keep.tile([P, PACK], F32, name="mag")
-        neg = keep.tile([P, PACK], F32, name="neg")
+        magnitude = keep.tile([P, PACK], F32, name="magnitude")
+        minus_two_if_negative = keep.tile([P, PACK], F32, name="minus_two_if_negative")
         sign = keep.tile([P, PACK], F32, name="sign")
-        nc.scalar.activation(mag[:], unit_sb[:], ACT.Abs)
-        nc.vector.tensor_scalar(neg[:], unit_sb[:], 0.0, -2.0, ALU.is_lt, ALU.mult)
-        nc.vector.tensor_scalar(sign[:], neg[:], 1.0, None, ALU.add)
+        nc.scalar.activation(magnitude[:], unit_sb[:], ACT.Abs)
+        nc.vector.tensor_scalar(minus_two_if_negative[:], unit_sb[:], 0.0, -2.0, ALU.is_lt, ALU.mult)
+        nc.vector.tensor_scalar(sign[:], minus_two_if_negative[:], 1.0, None, ALU.add)
 
-        def cast_pair(raw, name, half, copy):
-            g = keep.tile([P, 2, P, PACK], BF16, name="%s_bf%d" % (name, half), align_bytes=64)
+        def round_plane_pair(raw, name, pair, copy):
+            rounded = sbuf("%s_bf16_%d" % (name, pair), [2, P, PACK], BF16)
             copy(
-                g[:].rearrange("p t m j -> p m j t"),
-                raw[:].rearrange("p j (m h t) -> p h m j t", h=2, t=2)[:, half],
+                rounded[:].rearrange("p t m j -> p m j t"),
+                raw[:].rearrange("p j (m pair t) -> p pair m j t", pair=2, t=2)[:, pair],
             )
-            return g
+            return rounded[:].rearrange("p t m j -> p (t m j)")
 
-        def quantize(g_flat, width, name):
-            codes = keep.tile([P, width], U32, name=name + "_codes", align_bytes=64)
-            scales = keep.tile([P, width], U8, name=name + "_scales", align_bytes=64)
-            nc.vector.quantize_mx(out=codes[:].bitcast(FP8X4), scales=scales[:], in_=g_flat)
+        def quantize(values, name):
+            columns = values.shape[1] // PACK
+            codes = sbuf(name + "_codes", [columns], U32)
+            scales = sbuf(name + "_scales", [columns], U8)
+            nc.vector.quantize_mx(out=codes[:].bitcast(FP8X4), scales=scales[:], in_=values)
             return codes, scales
 
-        gs = keep.tile([P, S], U8, name="gs", align_bytes=64)
-        gw = keep.tile([P, S], U32, name="gw", align_bytes=64)
-        nc.vector.tensor_copy(gs[:], xs[:].indirect(offs_sb[:]))
-        g1 = [cast_pair(w1_raw, "w1", 0, nc.vector.tensor_copy), cast_pair(w1_raw, "w1", 1, nc.scalar.copy)]
-        q1 = [quantize(g[:].rearrange("p t m j -> p (t m j)"), 2 * P, "w1q%d" % h) for h, g in enumerate(g1)]
-        halves = [slice(h * S // X_PARTS, (h + 1) * S // X_PARTS) for h in range(X_PARTS)]
-        for cols in halves:
-            nc.vector.tensor_copy(gw[:, cols], xw[:].bitcast(U32).indirect(offs_sb[:, cols.start // LIST : cols.stop // LIST]))
+        def entries(list_sb, first, width):
+            return list_sb[:, first // LIST : (first + width) // LIST]
 
-        y = [keep.tile([P, Y_WINDOW], F32, name="y%d" % t, align_bytes=64) for t in range(PACK)]
-        z = [keep.tile([P, Z_WINDOW], F32, name="z%d" % t, align_bytes=64) for t in range(PACK)]
-        for win in y + z:
-            if win.shape[1] > S:
-                nc.gpsimd.memset(win[:, S:], 0.0)
-
-        def multiply(q, t, acc, part):
-            codes, scales = q[t // 2]
-            cols = slice((t % 2) * P, (t % 2 + 1) * P)
-            nc.tensor.matmul_mx(
-                out=acc[:, part], lhsT=codes[:, cols].bitcast(FP8X4), lhsT_scale=scales[:, cols],
-                rhs=gw[:, part].bitcast(FP8X4), rhs_scale=gs[:, part], start=True, stop=True,
+        x_picked_scales = sbuf("x_picked_scales", [S], U8)
+        x_picked = sbuf("x_picked", [S], U32)
+        nc.vector.tensor_copy(x_picked_scales[:], scale_table[:].indirect(offs_sb[:]))
+        w1_bf16 = [
+            round_plane_pair(w1_raw, "w1", 0, nc.vector.tensor_copy),
+            round_plane_pair(w1_raw, "w1", 1, nc.scalar.copy),
+        ]
+        w1_mx = [quantize(values, "w1_%d" % pair) for pair, values in enumerate(w1_bf16)]
+        halves = [slice(0, S // 2), slice(S // 2, S)]
+        for half in halves:
+            nc.vector.tensor_copy(
+                x_picked[:, half], x_table[:].bitcast(U32).indirect(entries(offs_sb, half.start, S // 2))
             )
 
-        def leave(acc, t, win, on_vector):
-            if on_vector:
-                nc.vector.tensor_scalar(win[:, :S], acc[:], mag[:, t : t + 1], None, ALU.mult)
+        y = [sbuf("y%d" % t, [S + GROUP], F32) for t in range(PACK)]
+        z = [sbuf("z%d" % t, [S], F32) for t in range(PACK)]
+        for window in y:
+            nc.gpsimd.memset(window[:, S:], 0.0)
+
+        def project(w_mx, t, acc, picked):
+            codes, scales = w_mx[t // 2]
+            plane = slice((t % 2) * P, (t % 2 + 1) * P)
+            nc.tensor.matmul_mx(
+                out=acc[:, picked],
+                lhsT=codes[:, plane].bitcast(FP8X4),
+                lhsT_scale=scales[:, plane],
+                rhs=x_picked[:, picked].bitcast(FP8X4),
+                rhs_scale=x_picked_scales[:, picked],
+                start=True,
+                stop=True,
+            )
+
+        def leave_psum(acc, t, window, on_scalar):
+            if on_scalar:
+                nc.scalar.activation(window[:, :S], acc[:], ACT.Copy, scale=magnitude[:, t : t + 1])
             else:
-                nc.scalar.activation(win[:, :S], acc[:], ACT.Copy, scale=mag[:, t : t + 1])
+                nc.vector.tensor_scalar(window[:, :S], acc[:], magnitude[:, t : t + 1], None, ALU.mult)
 
-        def work(name, c, w):
-            return keep.tile([P, PACK, w], F32, name="%s%d" % (name, c), align_bytes=64)
+        y_left = [sbuf("y_left%d" % g, [PACK, GROUP], F32) for g in range(len(Y_RANGES))]
+        diff = [sbuf("diff%d" % g, [PACK, GROUP], F32) for g in range(len(Y_RANGES))]
+        term = [sbuf("term%d" % g, [PACK, GROUP], F32) for g in range(len(Y_RANGES))]
 
-        def entries(lst, c0, w):
-            return lst[:, c0 // LIST : (c0 + w) // LIST]
-
-        n_ch = len(CHUNKS)
-        yl = [work("yl", g, w) for g, (c0, w) in enumerate(GROUPS)]
-        dif = [keep.tile([P, PACK, w], F32, name="dif%d" % g, tag="dif%d" % g, align_bytes=64) for g, (c0, w) in enumerate(GROUPS)]
-        term = [work("term", g, w) for g, (c0, w) in enumerate(GROUPS)]
-        zl, zr = [], []
-
-        def y_pairs(g):
-            c0, w = GROUPS[g]
+        def y_differences(g):
             for t in range(PACK):
-                nc.scalar.activation(yl[g][:, t, :], y[t][:].indirect(entries(l_sb, c0, w)), ACT.Copy)
-                nc.vector.tensor_tensor(dif[g][:, t, :], y[t][:].indirect(entries(r_sb, c0, w)), yl[g][:, t, :], ALU.subtract)
+                nc.scalar.activation(y_left[g][:, t, :], y[t][:].indirect(entries(left_sb, *Y_RANGES[g])), ACT.Copy)
+                nc.vector.tensor_tensor(
+                    diff[g][:, t, :], y[t][:].indirect(entries(right_sb, *Y_RANGES[g])), y_left[g][:, t, :], ALU.subtract
+                )
 
-        def magnitude(g):
-            nc.scalar.activation(term[g][:], dif[g][:], ACT.Abs)
+        def absolute(g):
+            nc.scalar.activation(term[g][:], diff[g][:], ACT.Abs)
 
         def times_length(g):
             nc.vector.tensor_tensor(term[g][:], term[g][:], bd_sb[g][:], ALU.mult)
 
-        def columns(tiles, ranges, c0, w):
-            k = [k for k, r in enumerate(ranges) if r[0] <= c0 < r[0] + r[1]][0]
-            return tiles[k][:, :, c0 - ranges[k][0] : c0 - ranges[k][0] + w]
+        def borders(tiles, ranges, first, width):
+            index = max(i for i, (start, count) in enumerate(ranges) if start <= first)
+            at = first - ranges[index][0]
+            return tiles[index][:, :, at : at + width]
 
-        def z_sides(u):
-            c0, w, f = UNITS[u]
+        def z_sides(index):
+            first, width = Z_RANGES[index]
             for t in range(PACK):
-                for dst, lst in ((zl, l_sb), (zr, r_sb)):
-                    win = z[t][:].indirect(entries(lst, c0, w))
-                    if f:
-                        nc.vector.tensor_tensor(dst[u][:, t, :], win, columns(term, GROUPS, c0, w)[:, t, :], ALU.add)
+                for side, list_sb in ((z_left, left_sb), (z_right, right_sb)):
+                    fetched = z[t][:].indirect(entries(list_sb, first, width))
+                    if first < FUSED:
+                        added = borders(term, Y_RANGES, first, width)[:, t, :]
+                        nc.vector.tensor_tensor(side[index][:, t, :], fetched, added, ALU.add)
                     else:
-                        nc.scalar.activation(dst[u][:, t, :], win, ACT.Copy)
+                        nc.scalar.activation(side[index][:, t, :], fetched, ACT.Copy)
 
-        hid = [keep.tile([P, w, PACK], BF16, name="hid%d" % c, align_bytes=64) for c, (c0, w) in enumerate(CHUNKS)]
+        hid = [sbuf("hid%d" % c, [width, PACK], BF16) for c, (first, width) in enumerate(OUT_RANGES)]
 
-        def combine(c, f):
-            c0, w = CHUNKS[c]
-            walk = "p t (c i) -> p c t i"
-            dst = hid[c][:].rearrange("p (c i) t -> p c t i", i=RUN)
-            left = columns(zl, UNITS, c0, w)
-            if f:
-                nc.vector.tensor_tensor(dst, left.rearrange(walk, i=RUN), columns(zr, UNITS, c0, w).rearrange(walk, i=RUN), ALU.min)
-            else:
-                nc.vector.tensor_tensor(left, left, columns(zr, UNITS, c0, w), ALU.min)
-                nc.vector.tensor_tensor(dst, left.rearrange(walk, i=RUN), columns(term, GROUPS, c0, w).rearrange(walk, i=RUN), ALU.add)
-
-        out_rows = out.rearrange("(h p) r -> p h r", p=P)
-
-        def finish(c):
-            c0, w = CHUNKS[c]
-            codes, scales = quantize(hid[c][:].rearrange("p r t -> p (r t)"), w, "hq%d" % c)
-            acc = out_psum.tile([P, 2, w], F32, name="oacc")
-            for h in range(2):
-                cols = slice(h * P, (h + 1) * P)
-                nc.tensor.matmul_mx(
-                    out=acc[:, h, :], lhsT=q3[0][:, cols].bitcast(FP8X4), lhsT_scale=q3[1][:, cols],
-                    rhs=codes[:].bitcast(FP8X4), rhs_scale=scales[:], start=True, stop=True,
+        def combine(c):
+            first, width = OUT_RANGES[c]
+            by_runs = "p t (c i) -> p c t i"
+            interleaved = hid[c][:].rearrange("p (c i) t -> p c t i", i=RUN)
+            left = borders(z_left, Z_RANGES, first, width)
+            right = borders(z_right, Z_RANGES, first, width)
+            if first < FUSED:
+                nc.vector.tensor_tensor(
+                    interleaved, left.rearrange(by_runs, i=RUN), right.rearrange(by_runs, i=RUN), ALU.min
                 )
-            res = keep.tile([P, 2, w], F32, name="res%d" % c, align_bytes=64)
-            if c in OUT_ON_VECTOR:
-                nc.vector.tensor_copy(res[:], acc[:])
             else:
-                nc.scalar.copy(res[:], acc[:])
-            nc.sync.dma_start(out=out_rows[:, :, c0 : c0 + w], in_=res[:])
+                nc.vector.tensor_tensor(left, left, right, ALU.min)
+                added = borders(term, Y_RANGES, first, width)
+                nc.vector.tensor_tensor(
+                    interleaved, left.rearrange(by_runs, i=RUN), added.rearrange(by_runs, i=RUN), ALU.add
+                )
 
-        accs = [proj_psum.tile([P, S], F32, name="acc") for t in range(PACK)]
-        for t in range(PACK):
-            for part in halves:
-                multiply(q1, t, accs[t], part)
-        g3 = keep.tile([P, N, PACK], BF16, name="w3_bf", align_bytes=64)
-        for t in range(PACK):
-            leave(accs[t], t, y[t], t in Y_ON_VECTOR)
-        y_pairs(0)
-        def prep3():
-            nc.vector.tensor_tensor(
-                g3[:].rearrange("p (c i) j -> p c j i", i=2),
-                w3_raw[:].rearrange("p j (c i) -> p c j i", i=2),
-                sign[:].unsqueeze(1).unsqueeze(3).broadcast_to([P, N // 2, PACK, 2]),
-                ALU.mult,
-            )
-            return quantize(g3[:].rearrange("p n j -> p (n j)"), N, "w3q")
+        out_halves = out.rearrange("(h p) r -> p h r", p=P)
 
-        if W3_FIRST:
-            q3 = prep3()
-        g2 = [cast_pair(w2_raw, "w2", 0, nc.vector.tensor_copy), cast_pair(w2_raw, "w2", 1, W2B)]
-        q2 = [quantize(g[:].rearrange("p t m j -> p (t m j)"), 2 * P, "w2q%d" % h) for h, g in enumerate(g2)]
+        def last_product(c):
+            first, width = OUT_RANGES[c]
+            codes, scales = quantize(hid[c][:].rearrange("p r t -> p (r t)"), "hid%d" % c)
+            acc = out_psum.tile([P, N // P, width], F32, name="out_acc")
+            for h in range(N // P):
+                rows = slice(h * P, (h + 1) * P)
+                nc.tensor.matmul_mx(
+                    out=acc[:, h, :],
+                    lhsT=w3_codes[:, rows].bitcast(FP8X4),
+                    lhsT_scale=w3_scales[:, rows],
+                    rhs=codes[:].bitcast(FP8X4),
+                    rhs_scale=scales[:],
+                    start=True,
+                    stop=True,
+                )
+            result = sbuf("result%d" % c, [N // P, width], F32)
+            nc.scalar.copy(result[:], acc[:])
+            nc.sync.dma_start(out=out_halves[:, :, first : first + width], in_=result[:])
+
+        y_acc = [proj_psum.tile([P, S], F32, name="proj_acc") for t in range(PACK)]
         for t in range(PACK):
-            acc = proj_psum.tile([P, S], F32, name="acc")
-            multiply(q2, t, acc, slice(0, S))
-            leave(acc, t, z[t], t in Z_ON_VECTOR)
-        magnitude(0)
-        y_pairs(1)
+            for half in halves:
+                project(w1_mx, t, y_acc[t], half)
+        w3_bf16 = sbuf("w3_bf16", [N, PACK], BF16)
+        for t in range(PACK):
+            leave_psum(y_acc[t], t, y[t], t == 0)
+        y_differences(0)
+
+        w2_bf16 = [round_plane_pair(w2_raw, "w2", pair, nc.vector.tensor_copy) for pair in range(2)]
+        w2_mx = [quantize(values, "w2_%d" % pair) for pair, values in enumerate(w2_bf16)]
+        for t in range(PACK):
+            z_acc = proj_psum.tile([P, S], F32, name="proj_acc")
+            project(w2_mx, t, z_acc, slice(0, S))
+            leave_psum(z_acc, t, z[t], t < Z_ON_SCALAR)
+
+        absolute(0)
+        y_differences(1)
         times_length(0)
-        if not W3_FIRST:
-            q3 = prep3()
-        magnitude(1)
-        fused = keep.tile([P, 2 * PACK * FUSED], F32, name="zf", align_bytes=64)
-        plain = keep.tile([P, 2 * PACK * (U - FUSED)], F32, name="zp", tag=PIN, align_bytes=64)
-        for u0, uw, f in UNITS:
-            base, at = (fused, u0) if f else (plain, u0 - FUSED)
-            at = 2 * PACK * at
-            zl.append(base[:, at : at + PACK * uw].rearrange("p (t r) -> p t r", t=PACK))
-            zr.append(base[:, at + PACK * uw : at + 2 * PACK * uw].rearrange("p (t r) -> p t r", t=PACK))
+        nc.vector.tensor_tensor(
+            w3_bf16[:].rearrange("p (c i) j -> p c j i", i=RUN),
+            w3_raw[:].rearrange("p j (c i) -> p c j i", i=RUN),
+            sign[:].unsqueeze(1).unsqueeze(3).broadcast_to([P, N // RUN, PACK, RUN]),
+            ALU.mult,
+        )
+        w3_codes, w3_scales = quantize(w3_bf16[:].rearrange("p n j -> p (n j)"), "w3")
+        absolute(1)
+
+        z_fused = sbuf("z_fused", [2 * PACK * FUSED], F32)
+        z_plain = sbuf("z_plain", [2 * PACK * (U - FUSED)], F32)
+        z_left, z_right = [], []
+        for first, width in Z_RANGES:
+            home, at = (z_fused, 2 * PACK * first) if first < FUSED else (z_plain, 2 * PACK * (first - FUSED))
+            size = PACK * width
+            z_left.append(home[:, at : at + size].rearrange("p (t r) -> p t r", t=PACK))
+            z_right.append(home[:, at + size : at + 2 * size].rearrange("p (t r) -> p t r", t=PACK))
+
         c = 0
-        for u, (u0, uw, f) in enumerate(UNITS):
-            z_sides(u)
-            if u == TERM_AT:
+        for index, (first, width) in enumerate(Z_RANGES):
+            z_sides(index)
+            if index == 0:
                 times_length(1)
-            while c < n_ch and CHUNKS[c][0] < u0 + uw:
-                combine(c, f)
+            while c < len(OUT_RANGES) and OUT_RANGES[c][0] < first + width:
+                combine(c)
                 if c > 0:
-                    finish(c - 1)
+                    last_product(c - 1)
                 c += 1
-        finish(n_ch - 1)
+        last_product(len(OUT_RANGES) - 1)

from contextlib import ExitStack

import concourse.mybir as mybir

K, T, S, N, H, U = 512, 2048, 512, 256, 512, 1024
FLOPS = 2 * (2 * K * H * S) + 2 * H * N * U

F32 = mybir.dt.float32
BF16 = mybir.dt.bfloat16
I32 = mybir.dt.int32
U32 = mybir.dt.uint32
U16 = mybir.dt.uint16
U8 = mybir.dt.uint8
FP8X4 = mybir.dt.float8_e4m3fn_x4
ALU = mybir.AluOpType
ACT = mybir.ActivationFunctionType

P = 128
PACK = 4
QUADRANT = 32
LIST = 16
RUN = 4

GROUP = 512
STEP = 256
LAST = 64
FUSED = 256
Z_ON_SCALAR = 3

Y_RANGES = [(first, GROUP) for first in range(0, U, GROUP)]
Z_RANGES = [(first, STEP) for first in range(0, U - STEP, STEP)] + [(U - STEP, STEP - LAST), (U - LAST, LAST)]
OUT_RANGES = Z_RANGES[:-2] + [(U - STEP, STEP - 2 * LAST), (U - 2 * LAST, LAST), (U - LAST, LAST)]


def tile_picked_ysegmrg_len_p_kernel(
    tc, x_words, x_scales, w1, w2, bd, unit, w3, offs, l1, r1, out
):
    nc = tc.nc
    with ExitStack() as ctx:
        lists = ctx.enter_context(tc.tile_pool(name="lists", bufs=1))
        keep = ctx.enter_context(tc.tile_pool(name="keep", bufs=1))
        proj_psum = ctx.enter_context(tc.psum_pool(name="proj_psum", bufs=PACK + 1))
        out_psum = ctx.enter_context(tc.psum_pool(name="out_psum", bufs=3))

        def sbuf(name, shape, dtype):
            return keep.tile([P] + shape, dtype, name=name, align_bytes=64)

        offs_sb = lists.tile([P, S // LIST], U16, name="offs_sb")
        left_sb = lists.tile([P, U // LIST], U16, name="left_sb")
        right_sb = lists.tile([P, U // LIST], U16, name="right_sb")
        x_table = sbuf("x_table", [T], I32)
        scale_table = sbuf("scale_table", [T], U8)
        w1_raw = sbuf("w1_raw", [PACK, H], F32)
        w2_raw = sbuf("w2_raw", [PACK, H], F32)
        w3_raw = sbuf("w3_raw", [PACK, N], F32)
        unit_sb = keep.tile([P, PACK], F32, name="unit_sb")
        bd_sb = [sbuf("bd%d" % g, [PACK, GROUP], F32) for g in range(len(Y_RANGES))]
        scale_rows = sbuf("scale_rows", [T // 4], I32)

        nc.vector.memset(scale_table[:].bitcast(I32), 0)
        live_rows = [slice(QUADRANT * q, QUADRANT * q + 4) for q in range(P // QUADRANT)]
        for q, rows in enumerate(live_rows):
            nc.sync.dma_start(out=scale_rows[rows, :], in_=x_scales[0, 4 * q : 4 * q + 4, :].bitcast(I32))
        nc.sync.dma_start(offs_sb[:], offs)
        nc.sync.dma_start(out=w1_raw[:], in_=w1.rearrange("(p j) c -> p j c", j=PACK))
        nc.sync.dma_start(out=x_table[:], in_=x_words[0].rearrange("p n j -> p (n j)").bitcast(I32))
        nc.scalar.dma_start(out=unit_sb[:], in_=unit.rearrange("(p t) o -> p (t o)", t=PACK))
        nc.sync.dma_start(left_sb[:], l1)
        nc.sync.dma_start(right_sb[:], r1)
        for rows in live_rows:
            nc.vector.tensor_copy(scale_table[rows, :].bitcast(I32), scale_rows[rows, :])
        nc.sync.dma_start(out=w2_raw[:], in_=w2.rearrange("(p j) c -> p j c", j=PACK))
        bd_planes = bd.rearrange("(p t) r -> p t r", t=PACK)
        nc.sync.dma_start(out=bd_sb[0][:], in_=bd_planes[:, :, :GROUP])
        nc.sync.dma_start(out=w3_raw[:], in_=w3.rearrange("(p j) c -> p j c", j=PACK))
        nc.sync.dma_start(out=bd_sb[1][:], in_=bd_planes[:, :, GROUP:])

        magnitude = keep.tile([P, PACK], F32, name="magnitude")
        minus_two_if_negative = keep.tile([P, PACK], F32, name="minus_two_if_negative")
        sign = keep.tile([P, PACK], F32, name="sign")
        nc.scalar.activation(magnitude[:], unit_sb[:], ACT.Abs)
        nc.vector.tensor_scalar(minus_two_if_negative[:], unit_sb[:], 0.0, -2.0, ALU.is_lt, ALU.mult)
        nc.vector.tensor_scalar(sign[:], minus_two_if_negative[:], 1.0, None, ALU.add)

        def round_plane_pair(raw, name, pair, copy):
            rounded = sbuf("%s_bf16_%d" % (name, pair), [2, P, PACK], BF16)
            copy(
                rounded[:].rearrange("p t m j -> p m j t"),
                raw[:].rearrange("p j (m pair t) -> p pair m j t", pair=2, t=2)[:, pair],
            )
            return rounded[:].rearrange("p t m j -> p (t m j)")

        def quantize(values, name):
            columns = values.shape[1] // PACK
            codes = sbuf(name + "_codes", [columns], U32)
            scales = sbuf(name + "_scales", [columns], U8)
            nc.vector.quantize_mx(out=codes[:].bitcast(FP8X4), scales=scales[:], in_=values)
            return codes, scales

        def entries(list_sb, first, width):
            return list_sb[:, first // LIST : (first + width) // LIST]

        x_picked_scales = sbuf("x_picked_scales", [S], U8)
        x_picked = sbuf("x_picked", [S], U32)
        nc.vector.tensor_copy(x_picked_scales[:], scale_table[:].indirect(offs_sb[:]))
        w1_bf16 = [
            round_plane_pair(w1_raw, "w1", 0, nc.vector.tensor_copy),
            round_plane_pair(w1_raw, "w1", 1, nc.scalar.copy),
        ]
        w1_mx = [quantize(values, "w1_%d" % pair) for pair, values in enumerate(w1_bf16)]
        halves = [slice(0, S // 2), slice(S // 2, S)]
        for half in halves:
            nc.vector.tensor_copy(
                x_picked[:, half], x_table[:].bitcast(U32).indirect(entries(offs_sb, half.start, S // 2))
            )

        y = [sbuf("y%d" % t, [S + GROUP], F32) for t in range(PACK)]
        z = [sbuf("z%d" % t, [S], F32) for t in range(PACK)]
        for window in y:
            nc.gpsimd.memset(window[:, S:], 0.0)

        def project(w_mx, t, acc, picked):
            codes, scales = w_mx[t // 2]
            plane = slice((t % 2) * P, (t % 2 + 1) * P)
            nc.tensor.matmul_mx(
                out=acc[:, picked],
                lhsT=codes[:, plane].bitcast(FP8X4),
                lhsT_scale=scales[:, plane],
                rhs=x_picked[:, picked].bitcast(FP8X4),
                rhs_scale=x_picked_scales[:, picked],
                start=True,
                stop=True,
            )

        def leave_psum(acc, t, window, on_scalar):
            if on_scalar:
                nc.scalar.activation(window[:, :S], acc[:], ACT.Copy, scale=magnitude[:, t : t + 1])
            else:
                nc.vector.tensor_scalar(window[:, :S], acc[:], magnitude[:, t : t + 1], None, ALU.mult)

        y_left = [sbuf("y_left%d" % g, [PACK, GROUP], F32) for g in range(len(Y_RANGES))]
        diff = [sbuf("diff%d" % g, [PACK, GROUP], F32) for g in range(len(Y_RANGES))]
        term = [sbuf("term%d" % g, [PACK, GROUP], F32) for g in range(len(Y_RANGES))]

        def y_differences(g):
            for t in range(PACK):
                nc.scalar.activation(y_left[g][:, t, :], y[t][:].indirect(entries(left_sb, *Y_RANGES[g])), ACT.Copy)
                nc.vector.tensor_tensor(
                    diff[g][:, t, :], y[t][:].indirect(entries(right_sb, *Y_RANGES[g])), y_left[g][:, t, :], ALU.subtract
                )

        def absolute(g):
            nc.scalar.activation(term[g][:], diff[g][:], ACT.Abs)

        def times_length(g):
            nc.vector.tensor_tensor(term[g][:], term[g][:], bd_sb[g][:], ALU.mult)

        def borders(tiles, ranges, first, width):
            index = max(i for i, (start, count) in enumerate(ranges) if start <= first)
            at = first - ranges[index][0]
            return tiles[index][:, :, at : at + width]

        def z_sides(index):
            first, width = Z_RANGES[index]
            for t in range(PACK):
                for side, list_sb in ((z_left, left_sb), (z_right, right_sb)):
                    fetched = z[t][:].indirect(entries(list_sb, first, width))
                    if first < FUSED:
                        added = borders(term, Y_RANGES, first, width)[:, t, :]
                        nc.vector.tensor_tensor(side[index][:, t, :], fetched, added, ALU.add)
                    else:
                        nc.scalar.activation(side[index][:, t, :], fetched, ACT.Copy)

        hid = [sbuf("hid%d" % c, [width, PACK], BF16) for c, (first, width) in enumerate(OUT_RANGES)]

        def combine(c):
            first, width = OUT_RANGES[c]
            by_runs = "p t (c i) -> p c t i"
            interleaved = hid[c][:].rearrange("p (c i) t -> p c t i", i=RUN)
            left = borders(z_left, Z_RANGES, first, width)
            right = borders(z_right, Z_RANGES, first, width)
            if first < FUSED:
                nc.vector.tensor_tensor(
                    interleaved, left.rearrange(by_runs, i=RUN), right.rearrange(by_runs, i=RUN), ALU.min
                )
            else:
                nc.vector.tensor_tensor(left, left, right, ALU.min)
                added = borders(term, Y_RANGES, first, width)
                nc.vector.tensor_tensor(
                    interleaved, left.rearrange(by_runs, i=RUN), added.rearrange(by_runs, i=RUN), ALU.add
                )

        out_halves = out.rearrange("(h p) r -> p h r", p=P)

        def last_product(c):
            first, width = OUT_RANGES[c]
            codes, scales = quantize(hid[c][:].rearrange("p r t -> p (r t)"), "hid%d" % c)
            acc = out_psum.tile([P, N // P, width], F32, name="out_acc")
            for h in range(N // P):
                rows = slice(h * P, (h + 1) * P)
                nc.tensor.matmul_mx(
                    out=acc[:, h, :],
                    lhsT=w3_codes[:, rows].bitcast(FP8X4),
                    lhsT_scale=w3_scales[:, rows],
                    rhs=codes[:].bitcast(FP8X4),
                    rhs_scale=scales[:],
                    start=True,
                    stop=True,
                )
            result = sbuf("result%d" % c, [N // P, width], F32)
            nc.scalar.copy(result[:], acc[:])
            nc.sync.dma_start(out=out_halves[:, :, first : first + width], in_=result[:])

        y_acc = [proj_psum.tile([P, S], F32, name="proj_acc") for t in range(PACK)]
        for t in range(PACK):
            for half in halves:
                project(w1_mx, t, y_acc[t], half)
        w3_bf16 = sbuf("w3_bf16", [N, PACK], BF16)
        for t in range(PACK):
            leave_psum(y_acc[t], t, y[t], t == 0)
        y_differences(0)

        w2_bf16 = [round_plane_pair(w2_raw, "w2", pair, nc.vector.tensor_copy) for pair in range(2)]
        w2_mx = [quantize(values, "w2_%d" % pair) for pair, values in enumerate(w2_bf16)]
        for t in range(PACK):
            z_acc = proj_psum.tile([P, S], F32, name="proj_acc")
            project(w2_mx, t, z_acc, slice(0, S))
            leave_psum(z_acc, t, z[t], t < Z_ON_SCALAR)

        absolute(0)
        y_differences(1)
        times_length(0)
        nc.vector.tensor_tensor(
            w3_bf16[:].rearrange("p (c i) j -> p c j i", i=RUN),
            w3_raw[:].rearrange("p j (c i) -> p c j i", i=RUN),
            sign[:].unsqueeze(1).unsqueeze(3).broadcast_to([P, N // RUN, PACK, RUN]),
            ALU.mult,
        )
        w3_codes, w3_scales = quantize(w3_bf16[:].rearrange("p n j -> p (n j)"), "w3")
        absolute(1)

        z_fused = sbuf("z_fused", [2 * PACK * FUSED], F32)
        z_plain = sbuf("z_plain", [2 * PACK * (U - FUSED)], F32)
        z_left, z_right = [], []
        for first, width in Z_RANGES:
            home, at = (z_fused, 2 * PACK * first) if first < FUSED else (z_plain, 2 * PACK * (first - FUSED))
            size = PACK * width
            z_left.append(home[:, at : at + size].rearrange("p (t r) -> p t r", t=PACK))
            z_right.append(home[:, at + size : at + 2 * size].rearrange("p (t r) -> p t r", t=PACK))

        c = 0
        for index, (first, width) in enumerate(Z_RANGES):
            z_sides(index)
            if index == 0:
                times_length(1)
            while c < len(OUT_RANGES) and OUT_RANGES[c][0] < first + width:
                combine(c)
                if c > 0:
                    last_product(c - 1)
                c += 1
        last_product(len(OUT_RANGES) - 1)
